import numpy as np
import ml_dtypes


def mxq(x, axis, fmt="e4m3"):
    dtype, down = {"e4m3": (ml_dtypes.float8_e4m3fn, 7), "e5m2": (ml_dtypes.float8_e5m2, 14)}[fmt]
    v = np.moveaxis(np.asarray(x, np.float32).astype(ml_dtypes.bfloat16).astype(np.float64), axis, -1)
    blocks = v.reshape(v.shape[:-1] + (-1, 32))
    amax = np.abs(blocks).max(-1, keepdims=True)
    byte = np.maximum(np.where(amax > 0, np.frexp(amax)[1] - 1 + 127, 0) - down, 1)
    scale = np.exp2(byte - 127.0)
    codes = (blocks / scale).astype(np.float32).astype(dtype).astype(np.float64)
    return np.moveaxis((codes * scale).reshape(v.shape), -1, axis)


WIDE = False


def mx_kscale(k):
    if not WIDE:
        return np.ones(k)
    levels = np.array([30, -30])
    if k % 512:
        return np.exp2(np.random.permutation(np.resize(levels, k // 32))).repeat(32)
    a = np.empty((k // 512, 16))
    for p in range(k // 512):
        a[p, :8] = np.random.permutation(np.resize(levels, 8))
        for g in range(8):
            far = levels[np.abs(levels - a[p, g]) >= 10]
            a[p, g + 8] = far[np.random.randint(len(far))]
    return np.exp2(a.ravel()).repeat(32)


def f64(x):
    return np.asarray(x).astype(np.float64)


def striped(idx):
    return np.tile(np.asarray(idx).reshape(-1, 16).T, (8, 1)).astype(np.uint16)


def unstriped(offs):
    return offs[:16].T.reshape(-1).astype(np.int64)


def striped8(idx):
    return np.asarray(idx).reshape(8, -1, 16).transpose(0, 2, 1).reshape(128, -1).astype(np.uint16)


def unstriped8(offs):
    return offs.reshape(8, 16, -1).transpose(0, 2, 1).reshape(8, -1).astype(np.int64)


def pick8(x, idx, run):
    r = np.arange(len(x))
    return x[r[:, None], idx[r % (8 * run) // run]]


E2M1 = np.array([0.0, 0.5, 1.0, 1.5, 2.0, 3.0, 4.0, 6.0, -0.0, -0.5, -1.0, -1.5, -2.0, -3.0, -4.0, -6.0])


def pack_weight(w, fmt):
    k, n = w.shape
    w = f64(np.asarray(w, np.float32).astype(ml_dtypes.bfloat16)).reshape(k // 32, 32, n)
    amax = np.abs(w).max(1)
    if fmt in ("e4m3", "e5m2"):
        byte = np.frexp(amax)[1] - 1 + 127 - (7 if fmt == "e4m3" else 14)
    else:
        mant, ex = np.frexp(amax / 6.0)
        byte = np.where(mant > 0.5, ex, ex - 1) + 127
    byte = np.clip(np.where(amax > 0, byte, 1), 1, 254)
    scaled = (w * np.exp2(127.0 - byte)[:, None, :]).reshape(k, n).astype(np.float32)
    by_word = np.ascontiguousarray(scaled.reshape(k // 512, 128, 4, n).transpose(0, 1, 3, 2))
    if fmt in ("e4m3", "e5m2"):
        words = by_word.astype(ml_dtypes.float8_e4m3fn if fmt == "e4m3" else ml_dtypes.float8_e5m2).view(np.uint8)
    else:
        c = by_word.astype(ml_dtypes.float4_e2m1fn).view(np.uint8) & 0xF
        words = (c[..., 0::2] | (c[..., 1::2] << 4)).reshape(k // 512, 128, 2 * n)
    return np.ascontiguousarray(words), np.ascontiguousarray(byte.astype(np.uint8).reshape(k // 512, 16, n))


def unpack_weight(words, scales, fmt):
    g, _, n = scales.shape
    words = np.ascontiguousarray(words).reshape(g, 128, n, -1)
    if fmt in ("e4m3", "e5m2"):
        vals = words.view(ml_dtypes.float8_e4m3fn if fmt == "e4m3" else ml_dtypes.float8_e5m2).astype(np.float64)
    else:
        nib = np.empty((g, 128, n, 4), np.uint8)
        nib[..., 0::2] = words & 0xF
        nib[..., 1::2] = words >> 4
        vals = E2M1[nib]
    vals = vals * np.repeat(np.exp2(scales.astype(np.float64) - 127.0), 8, axis=1)[..., None]
    return vals.transpose(0, 1, 3, 2).reshape(g * 512, n)


K, T, J, R, F, Z, C, I, O, N = 512, 1024, 256, 512, 512, 1024, 512, 128, 128, 256


def setup_inputs():
    n = np.random.standard_normal
    idx = np.random.permutation(T)[:J]
    idx2 = np.random.permutation(Z)[:J]
    idx3 = np.random.permutation(J)[:I]
    idx4 = np.stack([np.random.permutation(C)[:I] for _ in range(8)])
    idx5 = np.random.permutation(C)[:O]
    idx6 = np.random.permutation(J)[:O]
    idx7 = np.random.permutation(T)[:O]
    fk = mx_kscale(K)
    ff = mx_kscale(F)
    fr = mx_kscale(R)
    xtp = pack_weight(n((K, T)) / fk[:, None], "e2m1")
    xop = pack_weight(n((F, Z)) / ff[:, None], "e4m3")
    wp = pack_weight(n((K, R)) * 1 / np.sqrt(K) * fk[:, None] * fr, "e4m3")
    w2p = pack_weight(n((K, R)) * 1 / np.sqrt(K) * fk[:, None] * fr, "e5m2")
    w0p = pack_weight(n((F, R)) * 1 / np.sqrt(F) * ff[:, None] * fr, "e5m2")
    wbp = pack_weight(n((R, N)) * 1 / np.sqrt(R) / fr[:, None], "e2m1")
    wsp = pack_weight(n((K, N)) * 1 / np.sqrt(K) * fk[:, None], "e4m3")
    return {
        "xt_words": xtp[0],
        "xt_scales": xtp[1],
        "xo_words": xop[0],
        "xo_scales": xop[1],
        "w_words": wp[0],
        "w_scales": wp[1],
        "w2_words": w2p[0],
        "w2_scales": w2p[1],
        "w0_words": w0p[0],
        "w0_scales": w0p[1],
        "sa": (np.random.uniform(0.5, 1.6, (R, 1))).astype(np.float32),
        "sb": (np.random.uniform(0.5, 1.6, (R, 1))).astype(np.float32),
        "wb_words": wbp[0],
        "wb_scales": wbp[1],
        "ws_words": wsp[0],
        "ws_scales": wsp[1],
        "offs": striped(idx),
        "offs2": striped(idx2),
        "offs3": striped(idx3),
        "offs4": striped8(idx4),
        "offs5": striped(idx5),
        "offs6": striped(idx6),
        "offs7": striped(idx7),
    }


def reference(xt_words, xt_scales, xo_words, xo_scales, w_words, w_scales, w2_words, w2_scales, w0_words, w0_scales, sa, sb, wb_words, wb_scales, ws_words, ws_scales, offs, offs2, offs3, offs4, offs5, offs6, offs7):
    idx = unstriped(offs)
    idx2 = unstriped(offs2)
    idx3 = unstriped(offs3)
    idx4 = unstriped8(offs4)
    idx5 = unstriped(offs5)
    idx6 = unstriped(offs6)
    idx7 = unstriped(offs7)
    xtu = unpack_weight(xt_words, xt_scales, "e2m1")
    xou = unpack_weight(xo_words, xo_scales, "e4m3")
    wu = unpack_weight(w_words, w_scales, "e4m3")
    w2u = unpack_weight(w2_words, w2_scales, "e5m2")
    w0u = unpack_weight(w0_words, w0_scales, "e5m2")
    wbu = unpack_weight(wb_words, wb_scales, "e2m1")
    wsu = unpack_weight(ws_words, ws_scales, "e4m3")
    xtidxg = xtu[:, idx]
    a = wu.T @ xtidxg
    xoidx2g = xou[:, idx2]
    b = w2u.T @ xtidxg + w0u.T @ xoidx2g
    h1 = a[:, idx3] * f64(sa)
    pw = np.zeros((R, C))
    pw[np.arange(R)[:, None], idx4[np.arange(R) % 512 // 64]] = h1
    hid = np.abs(pw[:, idx5] - b[:, idx6] * f64(sb))
    hidq = mxq(hid, 0, "e5m2")
    xtidx7g = xtu[:, idx7]
    y = wbu.T @ hidq + wsu.T @ xtidx7g
    return y

@@ -1,0 +1,245 @@
+from contextlib import ExitStack
+
+import concourse.mybir as mybir
+
+K, T, J, R, F, Z, C, I, O, N = 512, 1024, 256, 512, 512, 1024, 512, 128, 128, 256
+FLOPS = 2 * (K * R * J * 2 + F * R * J + R * N * O + K * N * O)
+
+F32 = mybir.dt.float32
+BF16 = mybir.dt.bfloat16
+I32 = mybir.dt.int32
+U32 = mybir.dt.uint32
+U16 = mybir.dt.uint16
+U8 = mybir.dt.uint8
+E4M3 = mybir.dt.float8_e4m3fn_x4
+E5M2 = mybir.dt.float8_e5m2_x4
+E2M1 = mybir.dt.float4_e2m1fn_x4
+ACT = mybir.ActivationFunctionType
+ALU = mybir.AluOpType
+
+P = 128
+PACK = 4
+QUADS = 4
+
+
+def tile_list_ownseats_leaned_further_plain_kernel(
+    tc, xt_words, xt_scales, xo_words, xo_scales, w_words, w_scales, w2_words, w2_scales, w0_words, w0_scales,
+    sa, sb, wb_words, wb_scales, ws_words, ws_scales, offs, offs2, offs3, offs4, offs5, offs6, offs7, out,
+):
+    nc = tc.nc
+    with ExitStack() as ctx:
+        lists = ctx.enter_context(tc.tile_pool(name="lists", bufs=1))
+        sb_pool = ctx.enter_context(tc.tile_pool(name="work", bufs=1))
+        psum = ctx.enter_context(tc.psum_pool(name="psum", bufs=1))
+
+        def tile(name, shape, dtype):
+            return sb_pool.tile(shape, dtype, name=name, align_bytes=64)
+
+        def load_list(name, src):
+            t = lists.tile(list(src.shape), U16, name=name)
+            nc.sync.dma_start(t[:], src)
+            return t
+
+        def zero_plane(name, width):
+            t = tile(name, [P, width], U8)
+            nc.vector.memset(t[:].bitcast(I32), 0)
+            return t
+
+        def load_plane(queue, plane, src):
+            rows = src[0].bitcast(I32)
+            for q in range(QUADS):
+                queue.dma_start(plane[32 * q : 32 * q + 4, :].bitcast(I32), rows[4 * q : 4 * q + 4, :])
+
+        def stage_plane(name, src):
+            width = src.shape[2]
+            t = tile(name, [PACK, QUADS, width // 4], I32)
+            nc.sync.dma_start(t[:], src[0].bitcast(I32).rearrange("(q r) w -> r q w", r=4))
+            return t
+
+        def spread_plane(plane, staged):
+            for q in range(QUADS):
+                nc.vector.tensor_copy(plane[32 * q : 32 * q + 4, :].bitcast(I32), staged[:, q, :])
+
+        def load_words8(name, src):
+            width = src.shape[2]
+            t = tile(name, [P, width], U32)
+            nc.sync.dma_start(t[:].bitcast(I32), src[0].rearrange("p n t -> p (n t)").bitcast(I32))
+            return t
+
+        def load_words4(name, src):
+            t = tile(name, [P, src.shape[2] // 2], U16)
+            nc.sync.dma_start(t[:].bitcast(I32), src[0].bitcast(I32))
+            return t
+
+        def load_rows(name, src):
+            t = tile(name, [P, PACK], F32)
+            nc.gpsimd.dma_start(t[:], src.rearrange("(p t) one -> p (t one)", t=PACK))
+            return t
+
+        def deal_words(copy, name, words):
+            t = tile(name, [P, R], U32)
+            copy(
+                t[:].rearrange("p (t c i) -> p c t i", t=PACK, i=4),
+                words[:].rearrange("p (c i t) -> p c t i", t=PACK, i=4),
+            )
+            return t
+
+        def deal_plane(copy, name, plane):
+            t = tile(name, [P, R], U8)
+            copy(
+                t[:].rearrange("p (t m) -> p t m", t=PACK), plane[:].rearrange("p (m t) -> p t m", t=PACK)
+            )
+            return t
+
+        def gather(name, table, offsets, count, dtype):
+            t = tile(name, [P, count], dtype)
+            nc.vector.tensor_copy(t[:], table[:].indirect(offsets[:]))
+            return t
+
+        xt_pl = zero_plane("xt_pl", T)
+        w_pl = zero_plane("w_pl", R)
+        xo_pl = zero_plane("xo_pl", Z)
+        w2_pl = zero_plane("w2_pl", R)
+        w0_pl = zero_plane("w0_pl", R)
+        ws_pl = zero_plane("ws_pl", N)
+        wb_pl = zero_plane("wb_pl", N)
+
+        w_st = stage_plane("w_st", w_scales)
+        l1 = load_list("l1", offs)
+        xt_w = load_words4("xt_w", xt_words)
+        w_w = load_words8("w_w", w_words)
+        load_plane(nc.sync, xt_pl, xt_scales)
+        sa_t = load_rows("sa_t", sa)
+        sb_t = load_rows("sb_t", sb)
+        l3 = load_list("l3", offs3)
+        xo_w = load_words8("xo_w", xo_words)
+        w2_w = load_words8("w2_w", w2_words)
+        l4 = load_list("l4", offs4)
+        w0_w = load_words8("w0_w", w0_words)
+        l2 = load_list("l2", offs2)
+        l7 = load_list("l7", offs7)
+        l5 = load_list("l5", offs5)
+        load_plane(nc.sync, xo_pl, xo_scales)
+        load_plane(nc.sync, w2_pl, w2_scales)
+        load_plane(nc.sync, w0_pl, w0_scales)
+        l6 = load_list("l6", offs6)
+        ws_w = load_words8("ws_w", ws_words)
+        wb_w = load_words4("wb_w", wb_words)
+        load_plane(nc.sync, ws_pl, ws_scales)
+        load_plane(nc.sync, wb_pl, wb_scales)
+
+        boards = []
+        for t in range(PACK):
+            board = tile("board%d" % t, [P, C], F32)
+            (nc.gpsimd if t < 2 else nc.vector).memset(board[:], 0.0)
+            boards.append(board)
+
+        banks = [psum.tile([P, 2 * J], F32, name="bank%d" % t) for t in range(PACK)]
+        y_banks = [psum.tile([P, O], F32, name="ybank%d" % h) for h in range(N // P)]
+
+        spread_plane(w_pl, w_st)
+        xg_w = gather("xg_w", xt_w, l1, J, U16)
+        w_d = deal_words(nc.scalar.copy, "w_d", w_w)
+        w_ds = deal_plane(nc.vector.tensor_copy, "w_ds", w_pl)
+        xg_s = gather("xg_s", xt_pl, l1, J, U8)
+        a_rows = []
+        for t in range(PACK):
+            cols = slice(t * P, (t + 1) * P)
+            nc.tensor.matmul_mx(
+                out=banks[t][:, 0:J], lhsT=w_d[:, cols].bitcast(E4M3), lhsT_scale=w_ds[:, cols],
+                rhs=xg_w[:].bitcast(E2M1), rhs_scale=xg_s[:], start=True, stop=True,
+            )
+        for t in range(PACK):
+            a_t = tile("a%d" % t, [P, J], F32)
+            nc.vector.tensor_copy(a_t[:], banks[t][:, 0:J])
+            a_rows.append(a_t)
+
+        seats = [tile("seat%d" % t, [P, I], F32) for t in range(PACK)]
+
+        def fetch_a(t):
+            nc.scalar.activation(seats[t][:], a_rows[t][:].indirect(l3[:]), ACT.Copy, scale=sa_t[:, t : t + 1])
+
+        def put(t):
+            nc.scalar.activation(boards[t][:].indirect(l4[:]), seats[t][:], ACT.Copy)
+
+        fetch_a(0)
+        for t in range(1, PACK):
+            fetch_a(t)
+            put(t - 1)
+        put(PACK - 1)
+
+        og_w = gather("og_w", xo_w, l2, J, U32)
+        w2_d = deal_words(nc.gpsimd.tensor_copy, "w2_d", w2_w)
+        w0_d = deal_words(nc.gpsimd.tensor_copy, "w0_d", w0_w)
+        og_s = gather("og_s", xo_pl, l2, J, U8)
+        w2_ds = deal_plane(nc.gpsimd.tensor_copy, "w2_ds", w2_pl)
+        w0_ds = deal_plane(nc.vector.tensor_copy, "w0_ds", w0_pl)
+        for t in range(PACK):
+            cols = slice(t * P, (t + 1) * P)
+            nc.tensor.matmul_mx(
+                out=banks[t][:, J : 2 * J], lhsT=w2_d[:, cols].bitcast(E5M2), lhsT_scale=w2_ds[:, cols],
+                rhs=xg_w[:].bitcast(E2M1), rhs_scale=xg_s[:], start=True, stop=False,
+            )
+            nc.tensor.matmul_mx(
+                out=banks[t][:, J : 2 * J], lhsT=w0_d[:, cols].bitcast(E5M2), lhsT_scale=w0_ds[:, cols],
+                rhs=og_w[:].bitcast(E4M3), rhs_scale=og_s[:], start=False, stop=True,
+            )
+        b_rows = []
+        for t in range(PACK):
+            b_t = tile("b%d" % t, [P, J], F32)
+            nc.vector.tensor_copy(b_t[:], banks[t][:, J : 2 * J])
+            b_rows.append(b_t)
+
+        picked_b = tile("picked_b", [P, PACK, O], F32)
+        for t in range(PACK):
+            nc.scalar.activation(picked_b[:, t, :], b_rows[t][:].indirect(l6[:]), ACT.Copy, scale=sb_t[:, t : t + 1])
+
+        picked_pw = tile("picked_pw", [P, PACK, O], F32)
+        for t in range(PACK):
+            nc.vector.tensor_copy(picked_pw[:, t, :], boards[t][:].indirect(l5[:]))
+
+        sg_w = gather("sg_w", xt_w, l7, O, U16)
+        sg_s = gather("sg_s", xt_pl, l7, O, U8)
+        for h in range(N // P):
+            cols = slice(h * P, (h + 1) * P)
+            nc.tensor.matmul_mx(
+                out=y_banks[h][:], lhsT=ws_w[:, cols].bitcast(E4M3), lhsT_scale=ws_pl[:, cols],
+                rhs=sg_w[:].bitcast(E2M1), rhs_scale=sg_s[:], start=True, stop=False,
+            )
+
+        diff = tile("diff", [P, PACK, O], F32)
+        last = PACK - 1
+        nc.vector.tensor_tensor(diff[:, 0:last, :], picked_pw[:, 0:last, :], picked_b[:, 0:last, :], ALU.subtract)
+        nc.vector.tensor_tensor(diff[:, last, :], picked_pw[:, last, :], picked_b[:, last, :], ALU.subtract)
+
+        half = O // 2
+        hid_lo = tile("hid_lo", [P, half, PACK], BF16)
+        hid_hi = tile("hid_hi", [P, half, PACK], BF16)
+        nc.scalar.activation(
+            hid_lo[:].rearrange("p (c i) t -> p c t i", i=4),
+            diff[:, :, 0:half].rearrange("p t (c i) -> p c t i", i=4),
+            ACT.Abs,
+        )
+        hi = diff[:, :, half:O].rearrange("p t o -> p o t")
+        nc.vector.scalar_tensor_tensor(hid_hi[:], hi, -1.0, hi, ALU.mult, ALU.max)
+
+        hq_w = tile("hq_w", [P, O], U32)
+        hq_s = tile("hq_s", [P, O], U8)
+        for part, hid in enumerate((hid_lo, hid_hi)):
+            cols = slice(part * half, (part + 1) * half)
+            nc.vector.quantize_mx(
+                out=hq_w[:, cols].bitcast(E5M2), scales=hq_s[:, cols], in_=hid[:].rearrange("p o t -> p (o t)")
+            )
+
+        for h in range(N // P):
+            cols = slice(h * P, (h + 1) * P)
+            nc.tensor.matmul_mx(
+                out=y_banks[h][:], lhsT=wb_w[:, cols].bitcast(E2M1), lhsT_scale=wb_pl[:, cols],
+                rhs=hq_w[:].bitcast(E5M2), rhs_scale=hq_s[:], start=False, stop=True,
+            )
+        y0 = tile("y0", [P, O], F32)
+        y1 = tile("y1", [P, O], F32)
+        nc.vector.tensor_copy(y0[:], y_banks[0][:])
+        nc.sync.dma_start(out[0:P, :], y0[:])
+        nc.scalar.copy(y1[:], y_banks[1][:])
+        nc.scalar.dma_start(out[P : 2 * P, :], y1[:])

@@ -32,8 +32,8 @@ def tile_list_ownseats_leaned_further_plain_kernel(
         sb_pool = ctx.enter_context(tc.tile_pool(name="work", bufs=1))
         psum = ctx.enter_context(tc.psum_pool(name="psum", bufs=1))
 
-        def tile(name, shape, dtype):
-            return sb_pool.tile(shape, dtype, name=name, align_bytes=64)
+        def tile(name, shape, dtype, after=None):
+            return sb_pool.tile(shape, dtype, name=name, tag=after or name, align_bytes=64)
 
         def load_list(name, src):
             t = lists.tile(list(src.shape), U16, name=name)
@@ -84,15 +84,15 @@ def tile_list_ownseats_leaned_further_plain_kernel(
             )
             return t
 
-        def deal_plane(copy, name, plane):
-            t = tile(name, [P, R], U8)
+        def deal_plane(copy, name, plane, after=None):
+            t = tile(name, [P, R], U8, after)
             copy(
                 t[:].rearrange("p (t m) -> p t m", t=PACK), plane[:].rearrange("p (m t) -> p t m", t=PACK)
             )
             return t
 
-        def gather(name, table, offsets, count, dtype):
-            t = tile(name, [P, count], dtype)
+        def gather(name, table, offsets, count, dtype, after=None):
+            t = tile(name, [P, count], dtype, after)
             nc.vector.tensor_copy(t[:], table[:].indirect(offsets[:]))
             return t
 
@@ -112,16 +112,16 @@ def tile_list_ownseats_leaned_further_plain_kernel(
         sa_t = load_rows("sa_t", sa)
         sb_t = load_rows("sb_t", sb)
         l3 = load_list("l3", offs3)
-        xo_w = load_words8("xo_w", xo_words)
         w2_w = load_words8("w2_w", w2_words)
-        l4 = load_list("l4", offs4)
         w0_w = load_words8("w0_w", w0_words)
+        l4 = load_list("l4", offs4)
+        xo_w = load_words8("xo_w", xo_words)
         l2 = load_list("l2", offs2)
-        l7 = load_list("l7", offs7)
-        l5 = load_list("l5", offs5)
-        load_plane(nc.sync, xo_pl, xo_scales)
         load_plane(nc.sync, w2_pl, w2_scales)
+        l7 = load_list("l7", offs7)
+        load_plane(nc.sync, xo_pl, xo_scales)
         load_plane(nc.sync, w0_pl, w0_scales)
+        l5 = load_list("l5", offs5)
         l6 = load_list("l6", offs6)
         ws_w = load_words8("ws_w", ws_words)
         wb_w = load_words4("wb_w", wb_words)
@@ -142,6 +142,7 @@ def tile_list_ownseats_leaned_further_plain_kernel(
         w_d = deal_words(nc.scalar.copy, "w_d", w_w)
         w_ds = deal_plane(nc.vector.tensor_copy, "w_ds", w_pl)
         xg_s = gather("xg_s", xt_pl, l1, J, U8)
+        w2_d = deal_words(nc.scalar.copy, "w2_d", w2_w)
         a_rows = []
         for t in range(PACK):
             cols = slice(t * P, (t + 1) * P)
@@ -168,11 +169,10 @@ def tile_list_ownseats_leaned_further_plain_kernel(
             put(t - 1)
         put(PACK - 1)
 
-        og_w = gather("og_w", xo_w, l2, J, U32)
-        w2_d = deal_words(nc.gpsimd.tensor_copy, "w2_d", w2_w)
-        w0_d = deal_words(nc.gpsimd.tensor_copy, "w0_d", w0_w)
+        w0_d = deal_words(nc.vector.tensor_copy, "w0_d", w0_w)
+        w2_ds = deal_plane(nc.vector.tensor_copy, "w2_ds", w2_pl, after="w_ds")
+        og_w = gather("og_w", xo_w, l2, J, U32, after="w_d")
         og_s = gather("og_s", xo_pl, l2, J, U8)
-        w2_ds = deal_plane(nc.gpsimd.tensor_copy, "w2_ds", w2_pl)
         w0_ds = deal_plane(nc.vector.tensor_copy, "w0_ds", w0_pl)
         for t in range(PACK):
             cols = slice(t * P, (t + 1) * P)
@@ -180,6 +180,8 @@ def tile_list_ownseats_leaned_further_plain_kernel(
                 out=banks[t][:, J : 2 * J], lhsT=w2_d[:, cols].bitcast(E5M2), lhsT_scale=w2_ds[:, cols],
                 rhs=xg_w[:].bitcast(E2M1), rhs_scale=xg_s[:], start=True, stop=False,
             )
+        for t in range(PACK):
+            cols = slice(t * P, (t + 1) * P)
             nc.tensor.matmul_mx(
                 out=banks[t][:, J : 2 * J], lhsT=w0_d[:, cols].bitcast(E5M2), lhsT_scale=w0_ds[:, cols],
                 rhs=og_w[:].bitcast(E4M3), rhs_scale=og_s[:], start=False, stop=True,
@@ -194,9 +196,10 @@ def tile_list_ownseats_leaned_further_plain_kernel(
         for t in range(PACK):
             nc.scalar.activation(picked_b[:, t, :], b_rows[t][:].indirect(l6[:]), ACT.Copy, scale=sb_t[:, t : t + 1])
 
-        picked_pw = tile("picked_pw", [P, PACK, O], F32)
+        picked_lo = tile("picked_lo", [P, 2, O], F32, after="w0_pl")
+        picked_hi = tile("picked_hi", [P, 2, O], F32, after="w_d")
         for t in range(PACK):
-            nc.vector.tensor_copy(picked_pw[:, t, :], boards[t][:].indirect(l5[:]))
+            nc.vector.tensor_copy((picked_lo, picked_hi)[t // 2][:, t % 2, :], boards[t][:].indirect(l5[:]))
 
         sg_w = gather("sg_w", xt_w, l7, O, U16)
         sg_s = gather("sg_s", xt_pl, l7, O, U8)
@@ -208,9 +211,9 @@ def tile_list_ownseats_leaned_further_plain_kernel(
             )
 
         diff = tile("diff", [P, PACK, O], F32)
-        last = PACK - 1
-        nc.vector.tensor_tensor(diff[:, 0:last, :], picked_pw[:, 0:last, :], picked_b[:, 0:last, :], ALU.subtract)
-        nc.vector.tensor_tensor(diff[:, last, :], picked_pw[:, last, :], picked_b[:, last, :], ALU.subtract)
+        nc.vector.tensor_tensor(diff[:, 0:2, :], picked_lo[:], picked_b[:, 0:2, :], ALU.subtract)
+        for t in range(2, PACK):
+            nc.vector.tensor_tensor(diff[:, t, :], picked_hi[:, t - 2, :], picked_b[:, t, :], ALU.subtract)
 
         half = O // 2
         hid_lo = tile("hid_lo", [P, half, PACK], BF16)

@@ -131,7 +131,7 @@ def tile_list_ownseats_leaned_further_plain_kernel(
         boards = []
         for t in range(PACK):
             board = tile("board%d" % t, [P, C], F32)
-            (nc.gpsimd if t < 2 else nc.vector).memset(board[:], 0.0)
+            nc.vector.memset(board[:], 0.0)
             boards.append(board)
 
         banks = [psum.tile([P, 2 * J], F32, name="bank%d" % t) for t in range(PACK)]

@@ -73,7 +73,7 @@ def tile_list_ownseats_leaned_further_plain_kernel(
 
         def load_rows(name, src):
             t = tile(name, [P, PACK], F32)
-            nc.gpsimd.dma_start(t[:], src.rearrange("(p t) one -> p (t one)", t=PACK))
+            nc.sync.dma_start(t[:], src.rearrange("(p t) one -> p (t one)", t=PACK))
             return t
 
         def deal_words(copy, name, words):
@@ -109,30 +109,31 @@ def tile_list_ownseats_leaned_further_plain_kernel(
         xt_w = load_words4("xt_w", xt_words)
         w_w = load_words8("w_w", w_words)
         load_plane(nc.sync, xt_pl, xt_scales)
-        sa_t = load_rows("sa_t", sa)
-        sb_t = load_rows("sb_t", sb)
-        l3 = load_list("l3", offs3)
         w2_w = load_words8("w2_w", w2_words)
         w0_w = load_words8("w0_w", w0_words)
+        l3 = load_list("l3", offs3)
+        sa_t = load_rows("sa_t", sa)
         l4 = load_list("l4", offs4)
-        xo_w = load_words8("xo_w", xo_words)
         l2 = load_list("l2", offs2)
-        load_plane(nc.sync, w2_pl, w2_scales)
         l7 = load_list("l7", offs7)
+        xo_w = load_words8("xo_w", xo_words)
+        load_plane(nc.sync, w2_pl, w2_scales)
         load_plane(nc.sync, xo_pl, xo_scales)
         load_plane(nc.sync, w0_pl, w0_scales)
         l5 = load_list("l5", offs5)
         l6 = load_list("l6", offs6)
+        sb_t = load_rows("sb_t", sb)
         ws_w = load_words8("ws_w", ws_words)
         wb_w = load_words4("wb_w", wb_words)
         load_plane(nc.sync, ws_pl, ws_scales)
         load_plane(nc.sync, wb_pl, wb_scales)
 
-        boards = []
-        for t in range(PACK):
-            board = tile("board%d" % t, [P, C], F32)
+        def zero_board(name, after=None):
+            board = tile(name, [P, C], F32, after)
             nc.vector.memset(board[:], 0.0)
-            boards.append(board)
+            return board
+
+        boards = [zero_board("board0"), zero_board("board1"), zero_board("board2")]
 
         banks = [psum.tile([P, 2 * J], F32, name="bank%d" % t) for t in range(PACK)]
         y_banks = [psum.tile([P, O], F32, name="ybank%d" % h) for h in range(N // P)]
@@ -155,6 +156,7 @@ def tile_list_ownseats_leaned_further_plain_kernel(
             nc.vector.tensor_copy(a_t[:], banks[t][:, 0:J])
             a_rows.append(a_t)
 
+        boards.append(zero_board("board3", after="w_w"))
         seats = [tile("seat%d" % t, [P, I], F32) for t in range(PACK)]
 
         def fetch_a(t):
@@ -192,14 +194,17 @@ def tile_list_ownseats_leaned_further_plain_kernel(
             nc.vector.tensor_copy(b_t[:], banks[t][:, J : 2 * J])
             b_rows.append(b_t)
 
+        picked_2 = tile("picked_2", [P, O], F32)
+        nc.scalar.activation(picked_2[:], boards[2][:].indirect(l5[:]), ACT.Copy)
         picked_b = tile("picked_b", [P, PACK, O], F32)
         for t in range(PACK):
             nc.scalar.activation(picked_b[:, t, :], b_rows[t][:].indirect(l6[:]), ACT.Copy, scale=sb_t[:, t : t + 1])
 
         picked_lo = tile("picked_lo", [P, 2, O], F32, after="w0_pl")
-        picked_hi = tile("picked_hi", [P, 2, O], F32, after="w_d")
-        for t in range(PACK):
-            nc.vector.tensor_copy((picked_lo, picked_hi)[t // 2][:, t % 2, :], boards[t][:].indirect(l5[:]))
+        picked_3 = tile("picked_3", [P, O], F32, after="w_d")
+        for t in range(2):
+            nc.vector.tensor_copy(picked_lo[:, t, :], boards[t][:].indirect(l5[:]))
+        nc.vector.tensor_copy(picked_3[:], boards[3][:].indirect(l5[:]))
 
         sg_w = gather("sg_w", xt_w, l7, O, U16)
         sg_s = gather("sg_s", xt_pl, l7, O, U8)
@@ -212,8 +217,8 @@ def tile_list_ownseats_leaned_further_plain_kernel(
 
         diff = tile("diff", [P, PACK, O], F32)
         nc.vector.tensor_tensor(diff[:, 0:2, :], picked_lo[:], picked_b[:, 0:2, :], ALU.subtract)
-        for t in range(2, PACK):
-            nc.vector.tensor_tensor(diff[:, t, :], picked_hi[:, t - 2, :], picked_b[:, t, :], ALU.subtract)
+        nc.vector.tensor_tensor(diff[:, 2, :], picked_2[:], picked_b[:, 2, :], ALU.subtract)
+        nc.vector.tensor_tensor(diff[:, 3, :], picked_3[:], picked_b[:, 3, :], ALU.subtract)
 
         half = O // 2
         hid_lo = tile("hid_lo", [P, half, PACK], BF16)

from contextlib import ExitStack

import concourse.mybir as mybir

K, T, J, R, F, Z, C, I, O, N = 512, 1024, 256, 512, 512, 1024, 512, 128, 128, 256
FLOPS = 2 * (K * R * J * 2 + F * R * J + R * N * O + K * N * O)

F32 = mybir.dt.float32
BF16 = mybir.dt.bfloat16
I32 = mybir.dt.int32
U32 = mybir.dt.uint32
U16 = mybir.dt.uint16
U8 = mybir.dt.uint8
E4M3 = mybir.dt.float8_e4m3fn_x4
E5M2 = mybir.dt.float8_e5m2_x4
E2M1 = mybir.dt.float4_e2m1fn_x4
ACT = mybir.ActivationFunctionType
ALU = mybir.AluOpType

P = 128
PACK = 4
QUADS = 4


def tile_list_ownseats_leaned_further_plain_kernel(
    tc, xt_words, xt_scales, xo_words, xo_scales, w_words, w_scales, w2_words, w2_scales, w0_words, w0_scales,
    sa, sb, wb_words, wb_scales, ws_words, ws_scales, offs, offs2, offs3, offs4, offs5, offs6, offs7, out,
):
    nc = tc.nc
    with ExitStack() as ctx:
        lists = ctx.enter_context(tc.tile_pool(name="lists", bufs=1))
        sb_pool = ctx.enter_context(tc.tile_pool(name="work", bufs=1))
        psum = ctx.enter_context(tc.psum_pool(name="psum", bufs=1))

        def tile(name, shape, dtype, after=None):
            return sb_pool.tile(shape, dtype, name=name, tag=after or name, align_bytes=64)

        def load_list(name, src):
            t = lists.tile(list(src.shape), U16, name=name)
            nc.sync.dma_start(t[:], src)
            return t

        def zero_plane(name, width):
            t = tile(name, [P, width], U8)
            nc.vector.memset(t[:].bitcast(I32), 0)
            return t

        def load_plane(queue, plane, src):
            rows = src[0].bitcast(I32)
            for q in range(QUADS):
                queue.dma_start(plane[32 * q : 32 * q + 4, :].bitcast(I32), rows[4 * q : 4 * q + 4, :])

        def stage_plane(name, src):
            width = src.shape[2]
            t = tile(name, [PACK, QUADS, width // 4], I32)
            nc.sync.dma_start(t[:], src[0].bitcast(I32).rearrange("(q r) w -> r q w", r=4))
            return t

        def spread_plane(plane, staged):
            for q in range(QUADS):
                nc.vector.tensor_copy(plane[32 * q : 32 * q + 4, :].bitcast(I32), staged[:, q, :])

        def load_words8(name, src):
            width = src.shape[2]
            t = tile(name, [P, width], U32)
            nc.sync.dma_start(t[:].bitcast(I32), src[0].rearrange("p n t -> p (n t)").bitcast(I32))
            return t

        def load_words4(name, src):
            t = tile(name, [P, src.shape[2] // 2], U16)
            nc.sync.dma_start(t[:].bitcast(I32), src[0].bitcast(I32))
            return t

        def load_rows(name, src):
            t = tile(name, [P, PACK], F32)
            nc.sync.dma_start(t[:], src.rearrange("(p t) one -> p (t one)", t=PACK))
            return t

        def deal_words(copy, name, words):
            t = tile(name, [P, R], U32)
            copy(
                t[:].rearrange("p (t c i) -> p c t i", t=PACK, i=4),
                words[:].rearrange("p (c i t) -> p c t i", t=PACK, i=4),
            )
            return t

        def deal_plane(copy, name, plane, after=None):
            t = tile(name, [P, R], U8, after)
            copy(
                t[:].rearrange("p (t m) -> p t m", t=PACK), plane[:].rearrange("p (m t) -> p t m", t=PACK)
            )
            return t

        def gather(name, table, offsets, count, dtype, after=None):
            t = tile(name, [P, count], dtype, after)
            nc.vector.tensor_copy(t[:], table[:].indirect(offsets[:]))
            return t

        xt_pl = zero_plane("xt_pl", T)
        w_pl = zero_plane("w_pl", R)
        xo_pl = zero_plane("xo_pl", Z)
        w2_pl = zero_plane("w2_pl", R)
        w0_pl = zero_plane("w0_pl", R)
        ws_pl = zero_plane("ws_pl", N)
        wb_pl = zero_plane("wb_pl", N)

        w_st = stage_plane("w_st", w_scales)
        l1 = load_list("l1", offs)
        xt_w = load_words4("xt_w", xt_words)
        w_w = load_words8("w_w", w_words)
        load_plane(nc.sync, xt_pl, xt_scales)
        w2_w = load_words8("w2_w", w2_words)
        w0_w = load_words8("w0_w", w0_words)
        l3 = load_list("l3", offs3)
        sa_t = load_rows("sa_t", sa)
        l4 = load_list("l4", offs4)
        l2 = load_list("l2", offs2)
        l7 = load_list("l7", offs7)
        xo_w = load_words8("xo_w", xo_words)
        load_plane(nc.sync, w2_pl, w2_scales)
        load_plane(nc.sync, xo_pl, xo_scales)
        load_plane(nc.sync, w0_pl, w0_scales)
        l5 = load_list("l5", offs5)
        l6 = load_list("l6", offs6)
        sb_t = load_rows("sb_t", sb)
        ws_w = load_words8("ws_w", ws_words)
        wb_w = load_words4("wb_w", wb_words)
        load_plane(nc.sync, ws_pl, ws_scales)
        load_plane(nc.sync, wb_pl, wb_scales)

        def zero_board(name, after=None):
            board = tile(name, [P, C], F32, after)
            nc.vector.memset(board[:], 0.0)
            return board

        boards = [zero_board("board0"), zero_board("board1"), zero_board("board2")]

        banks = [psum.tile([P, 2 * J], F32, name="bank%d" % t) for t in range(PACK)]
        y_banks = [psum.tile([P, O], F32, name="ybank%d" % h) for h in range(N // P)]

        spread_plane(w_pl, w_st)
        xg_w = gather("xg_w", xt_w, l1, J, U16)
        w_d = deal_words(nc.scalar.copy, "w_d", w_w)
        w_ds = deal_plane(nc.vector.tensor_copy, "w_ds", w_pl)
        xg_s = gather("xg_s", xt_pl, l1, J, U8)
        w2_d = deal_words(nc.scalar.copy, "w2_d", w2_w)
        a_rows = []
        for t in range(PACK):
            cols = slice(t * P, (t + 1) * P)
            nc.tensor.matmul_mx(
                out=banks[t][:, 0:J], lhsT=w_d[:, cols].bitcast(E4M3), lhsT_scale=w_ds[:, cols],
                rhs=xg_w[:].bitcast(E2M1), rhs_scale=xg_s[:], start=True, stop=True,
            )
        for t in range(PACK):
            a_t = tile("a%d" % t, [P, J], F32)
            nc.vector.tensor_copy(a_t[:], banks[t][:, 0:J])
            a_rows.append(a_t)

        boards.append(zero_board("board3", after="w_w"))
        seats = [tile("seat%d" % t, [P, I], F32) for t in range(PACK)]

        def fetch_a(t):
            nc.scalar.activation(seats[t][:], a_rows[t][:].indirect(l3[:]), ACT.Copy, scale=sa_t[:, t : t + 1])

        def put(t):
            nc.scalar.activation(boards[t][:].indirect(l4[:]), seats[t][:], ACT.Copy)

        fetch_a(0)
        for t in range(1, PACK):
            fetch_a(t)
            put(t - 1)
        put(PACK - 1)

        w0_d = deal_words(nc.vector.tensor_copy, "w0_d", w0_w)
        w2_ds = deal_plane(nc.vector.tensor_copy, "w2_ds", w2_pl, after="w_ds")
        og_w = gather("og_w", xo_w, l2, J, U32, after="w_d")
        og_s = gather("og_s", xo_pl, l2, J, U8)
        w0_ds = deal_plane(nc.vector.tensor_copy, "w0_ds", w0_pl)
        for t in range(PACK):
            cols = slice(t * P, (t + 1) * P)
            nc.tensor.matmul_mx(
                out=banks[t][:, J : 2 * J], lhsT=w2_d[:, cols].bitcast(E5M2), lhsT_scale=w2_ds[:, cols],
                rhs=xg_w[:].bitcast(E2M1), rhs_scale=xg_s[:], start=True, stop=False,
            )
        for t in range(PACK):
            cols = slice(t * P, (t + 1) * P)
            nc.tensor.matmul_mx(
                out=banks[t][:, J : 2 * J], lhsT=w0_d[:, cols].bitcast(E5M2), lhsT_scale=w0_ds[:, cols],
                rhs=og_w[:].bitcast(E4M3), rhs_scale=og_s[:], start=False, stop=True,
            )
        b_rows = []
        for t in range(PACK):
            b_t = tile("b%d" % t, [P, J], F32)
            nc.vector.tensor_copy(b_t[:], banks[t][:, J : 2 * J])
            b_rows.append(b_t)

        picked_2 = tile("picked_2", [P, O], F32)
        nc.scalar.activation(picked_2[:], boards[2][:].indirect(l5[:]), ACT.Copy)
        picked_b = tile("picked_b", [P, PACK, O], F32)
        for t in range(PACK):
            nc.scalar.activation(picked_b[:, t, :], b_rows[t][:].indirect(l6[:]), ACT.Copy, scale=sb_t[:, t : t + 1])

        picked_lo = tile("picked_lo", [P, 2, O], F32, after="w0_pl")
        picked_3 = tile("picked_3", [P, O], F32, after="w_d")
        for t in range(2):
            nc.vector.tensor_copy(picked_lo[:, t, :], boards[t][:].indirect(l5[:]))
        nc.vector.tensor_copy(picked_3[:], boards[3][:].indirect(l5[:]))

        sg_w = gather("sg_w", xt_w, l7, O, U16)
        sg_s = gather("sg_s", xt_pl, l7, O, U8)
        for h in range(N // P):
            cols = slice(h * P, (h + 1) * P)
            nc.tensor.matmul_mx(
                out=y_banks[h][:], lhsT=ws_w[:, cols].bitcast(E4M3), lhsT_scale=ws_pl[:, cols],
                rhs=sg_w[:].bitcast(E2M1), rhs_scale=sg_s[:], start=True, stop=False,
            )

        diff = tile("diff", [P, PACK, O], F32)
        nc.vector.tensor_tensor(diff[:, 0:2, :], picked_lo[:], picked_b[:, 0:2, :], ALU.subtract)
        nc.vector.tensor_tensor(diff[:, 2, :], picked_2[:], picked_b[:, 2, :], ALU.subtract)
        nc.vector.tensor_tensor(diff[:, 3, :], picked_3[:], picked_b[:, 3, :], ALU.subtract)

        half = O // 2
        hid_lo = tile("hid_lo", [P, half, PACK], BF16)
        hid_hi = tile("hid_hi", [P, half, PACK], BF16)
        nc.scalar.activation(
            hid_lo[:].rearrange("p (c i) t -> p c t i", i=4),
            diff[:, :, 0:half].rearrange("p t (c i) -> p c t i", i=4),
            ACT.Abs,
        )
        hi = diff[:, :, half:O].rearrange("p t o -> p o t")
        nc.vector.scalar_tensor_tensor(hid_hi[:], hi, -1.0, hi, ALU.mult, ALU.max)

        hq_w = tile("hq_w", [P, O], U32)
        hq_s = tile("hq_s", [P, O], U8)
        for part, hid in enumerate((hid_lo, hid_hi)):
            cols = slice(part * half, (part + 1) * half)
            nc.vector.quantize_mx(
                out=hq_w[:, cols].bitcast(E5M2), scales=hq_s[:, cols], in_=hid[:].rearrange("p o t -> p (o t)")
            )

        for h in range(N // P):
            cols = slice(h * P, (h + 1) * P)
            nc.tensor.matmul_mx(
                out=y_banks[h][:], lhsT=wb_w[:, cols].bitcast(E2M1), lhsT_scale=wb_pl[:, cols],
                rhs=hq_w[:].bitcast(E5M2), rhs_scale=hq_s[:], start=False, stop=True,
            )
        y0 = tile("y0", [P, O], F32)
        y1 = tile("y1", [P, O], F32)
        nc.vector.tensor_copy(y0[:], y_banks[0][:])
        nc.sync.dma_start(out[0:P, :], y0[:])
        nc.scalar.copy(y1[:], y_banks[1][:])
        nc.scalar.dma_start(out[P : 2 * P, :], y1[:])
